import numpy as np, ml_dtypes
CORES = [34,162,290,418,42,426]
N = 6
TK = 256
WID = [224,96,128,256,256,32]
def setup_inputs(rng):
    return {"x": rng.standard_normal((N, 128, TK), dtype=np.float32).astype(ml_dtypes.bfloat16), "w": rng.standard_normal((N, 128, 128), dtype=np.float32).astype(ml_dtypes.bfloat16)}
def setup_inputs_big(rng):
    d = setup_inputs(rng)
    for k in ("x", "w"): d[k] = (d[k].astype(np.float32) * 1024.0).astype(d[k].dtype)
    return d
def setup_inputs_small(rng):
    d = setup_inputs(rng)
    for k in ("x", "w"): d[k] = (d[k].astype(np.float32) * (1 / 1024.0)).astype(d[k].dtype)
    return d
def setup_inputs_apart(rng):
    d = setup_inputs(rng)
    f = (10.0 ** rng.permutation(np.linspace(-1.5, 1.5, N))).astype(np.float32).reshape(N, 1, 1)
    for k in ("x", "w"): d[k] = (d[k].astype(np.float32) * f).astype(d[k].dtype)
    return d
def setup_inputs_neg(rng):
    d = setup_inputs(rng)
    d["x"] = (np.abs(d["x"].astype(np.float32)) * 1048576.0).astype(d["x"].dtype); d["w"] = (-np.abs(d["w"].astype(np.float32))).astype(d["w"].dtype)
    return d
def whole(x, w):
    X, W = x.astype(np.float64), w.astype(np.float64)
    y = np.stack([np.max([W[j].T @ X[r] for j in range(N)], axis=0) for r in range(N)])
    return {"y": y.astype(ml_dtypes.bfloat16)}
def reference(x, w):
    o = whole(x, w)["y"].copy()
    for r in range(N):
        o[r][:, WID[r]:] = np.nan
    return {"y": o}

@@ -1,0 +1,206 @@
+from concourse.bass import DstId, RemoteDMATransfer
+from concourse.mybir import AluOpType
+
+N, M, TK = 6, 128, 256
+
+SCRATCH = {
+    "cat": ("sbuf", [128, M + M + TK], "bfloat16"),
+    "wl": ("sbuf", [128, N * M], "bfloat16"),
+    "pacc": ("sbuf", [128, M], "bfloat16"),
+    "pland": ("sbuf", [128, M], "bfloat16"),
+    "acc": ("sbuf", [128, TK], "bfloat16"),
+}
+for _j in range(N):
+    SCRATCH["ps%d" % _j] = ("psum", [128, 512], "float32")
+
+SEMAPHORES = ["ldw", "ldx", "sent", "pa", "vp", "vo", "st"] + ["a%d" % j for j in range(N)] + ["m%d" % j for j in range(N)]
+
+
+def _pop(mask):
+    return bin(mask).count("1")
+
+
+def _split(mask, k):
+    es = [e for e in range(mask.bit_length()) if (mask >> e) & 1]
+    per = 1
+    while per * 2 * k <= len(es):
+        per *= 2
+    return [sum(1 << e for e in es[i * per:(i + 1) * per]) for i in range(k)]
+
+
+def _plan(cores, wid, topo):
+    n = len(cores)
+    R = range(n)
+    near = [[a != b and topo.may_write(cores[a], cores[b]) and topo.may_write(cores[b], cores[a]) for b in R] for a in R]
+
+    def links(a, b):
+        ca, cb = cores[a], cores[b]
+        if topo.mates(ca, cb) or topo.same_plane(ca, cb):
+            return 1
+        if topo.rack(topo.host(ca)) != topo.rack(topo.host(cb)) and topo.chip(ca) == topo.chip(cb):
+            return 1
+        return 2
+
+    narrow = [r for r in R if wid[r] <= M]
+    wide = [r for r in R if wid[r] > M]
+    far = dict((b, [j for j in R if j != b and not near[j][b]]) for b in wide)
+    best = [None, None]
+
+    def match(i, used, cost, pairs):
+        if i == len(narrow):
+            if best[0] is None or cost < best[0]:
+                best[0], best[1] = cost, list(pairs)
+            return
+        s = narrow[i]
+        for b in wide:
+            if b in used or not near[b][s] or any(not near[f][s] for f in far[b]):
+                continue
+            match(i + 1, used + [b], cost + links(b, s), pairs + [(s, b)])
+
+    match(0, [], 0, [])
+    assert best[1] is not None and len(narrow) == len(wide)
+    partner = {}
+    for s, b in best[1]:
+        partner[s], partner[b] = b, s
+
+    calls = {}
+    for j in R:
+        relay = [s for s in narrow if s != j and j in far[partner[s]]]
+        plain = [b for b in wide if b != j and near[j][b] and not (j in narrow and partner[j] == b)]
+        plain.sort(key=lambda d: links(j, d))
+        tg = relay + plain
+        cj = []
+        if j in narrow:
+            cj.append([("cat", 0, M + wid[j], [partner[j]], topo.mask(cores[j], cores[partner[j]]))])
+            src = ("cat", 0, M)
+        else:
+            src = ("wl", j * M, (j + 1) * M)
+        common = topo.mask(cores[j], cores[tg[0]])
+        for d in tg:
+            common &= topo.mask(cores[j], cores[d])
+        cj.append([(src[0], src[1], src[2], [d], mk) for d, mk in zip(tg, _split(common, len(tg)))])
+        calls[j] = cj
+    return dict(near=near, links=links, narrow=narrow, wide=wide, far=far, partner=partner, calls=calls)
+
+
+def rank_program(g, core, T, topo):
+    r = T.rank_of(core)
+    if r is None:
+        return
+    cores, wid = list(T.cores), list(T.tables["WID"])
+    P = _plan(cores, wid, topo)
+    sem, partner, calls = T.sem, P["partner"], P["calls"]
+    wr, p = wid[r], partner[r]
+    is_narrow = r in P["narrow"]
+    te, ve = g.tensor, g.vector
+
+    def arr(j):
+        return sem["a%d" % j]
+
+    def slot(j):
+        return T.wl[:, j * M:(j + 1) * M]
+
+    def inc1(j):
+        return sum(_pop(t[4]) for c in calls[j] for t in c if r in t[3])
+
+    def dst_id(d):
+        rid, pid = topo.addr(cores[d], core)
+        return DstId(rid=rid, pnc=pid)
+
+    sent = [0]
+
+    def round1():
+        for c in calls[r]:
+            trs = []
+            for buf, c0, c1, ds, mk in c:
+                whole = buf == "cat" and c1 > M
+                out = T.cat[:, c0:c1] if whole else slot(r)
+                trs.append(RemoteDMATransfer(dst_ids=[dst_id(d) for d in ds], dma_engine_mask=mk, remote_sem=arr(r),
+                                             srcs=[T[buf][:, c0:c1]], dsts=[out for d in ds], alu_op=0))
+                sent[0] += _pop(mk)
+            g.remote_dma_fused(trs, local_sem=sem.sent)
+
+    def round2(out_ap, in_ap, rsem):
+        rid, pid = topo.addr(cores[p], core)
+        mk = topo.mask(core, cores[p])
+        g.remote_dma(out_ap, in_ap, rsem, sem.sent, pid, rid, mk)
+        sent[0] += _pop(mk)
+
+    inc2 = _pop(topo.mask(cores[p], core))
+
+    def fold(out, ps_ap, chain, k):
+        if k == 0:
+            ve.tensor_copy(out, ps_ap).then_inc(chain, 1)
+        else:
+            ve.wait_ge(chain, k)
+            ve.tensor_tensor(out, ps_ap, out, AluOpType.max).then_inc(chain, 1)
+
+    if is_narrow:
+        rel = P["far"][p]
+        g.sync.dma_start(T.cat[:, 0:M], T.w[:, :]).then_inc(sem.ldw, 16)
+        g.scalar.dma_start(T.cat[:, M:M + wr], T.x[:, 0:wr]).then_inc(sem.ldx, 16)
+        g.wait_ge(sem.ldw, 16)
+        g.wait_ge(sem.ldx, 16)
+        round1()
+        for f in rel:
+            g.wait_ge(arr(f), inc1(f))
+            round2(slot(f), slot(f), arr(f))
+        x = T.cat[:, M:M + wr]
+        te.wait_ge(sem.ldw, 16)
+        te.wait_ge(sem.ldx, 16)
+        te.matmul(T["ps%d" % r][:, 0:wr], T.cat[:, 0:M], x, start=True, stop=True).then_inc(sem["m%d" % r], 1)
+        for f in rel:
+            te.wait_ge(arr(f), inc1(f))
+            te.matmul(T["ps%d" % f][:, 0:wr], slot(f), x, start=True, stop=True).then_inc(sem["m%d" % f], 1)
+        k = 0
+        for j in [r] + rel:
+            ve.wait_ge(sem["m%d" % j], 1)
+            fold(T.acc[:, 0:wr], T["ps%d" % j][:, 0:wr], sem.vo, k)
+            k += 1
+        ve.wait_ge(sem.pa, inc2)
+        fold(T.acc[:, 0:wr], T.pland[:, 0:wr], sem.vo, k)
+        k += 1
+    else:
+        ws = wid[p]
+        far = P["far"][r]
+        g.sync.dma_start(slot(r), T.w[:, :]).then_inc(sem.ldw, 16)
+        g.scalar.dma_start(T.cat[:, M + ws:M + ws + wr], T.x[:, 0:wr]).then_inc(sem.ldx, 16)
+        g.wait_ge(sem.ldw, 16)
+        round1()
+        oth = [j for j in range(len(cores)) if j not in (r, p) and j not in far]
+        oth.sort(key=lambda j: (j in P["narrow"], P["links"](j, r)))
+        both = T.cat[:, M:M + ws + wr]
+        own = T.cat[:, M + ws:M + ws + wr]
+        te.wait_ge(sem.ldw, 16)
+        te.wait_ge(sem.ldx, 16)
+        te.wait_ge(arr(p), inc1(p))
+        te.matmul(T["ps%d" % r][:, 0:ws + wr], slot(r), both, start=True, stop=True).then_inc(sem["m%d" % r], 1)
+        te.matmul(T["ps%d" % p][:, ws:ws + wr], T.cat[:, 0:M], own, start=True, stop=True).then_inc(sem["m%d" % p], 1)
+        for j in oth:
+            te.wait_ge(arr(j), inc1(j))
+            te.matmul(T["ps%d" % j][:, 0:ws + wr], slot(j), both, start=True, stop=True).then_inc(sem["m%d" % j], 1)
+        for f in far:
+            te.wait_ge(arr(f), inc2)
+            te.matmul(T["ps%d" % f][:, ws:ws + wr], slot(f), own, start=True, stop=True).then_inc(sem["m%d" % f], 1)
+        seq = [("p", r), ("o", r), ("o", p)]
+        for j in oth[:-2]:
+            seq += [("p", j), ("o", j)]
+        seq += [("p", j) for j in oth[-2:]] + [("o", j) for j in oth[-2:]] + [("o", f) for f in far]
+        kp, k, seen = 0, 0, []
+        for kind, j in seq:
+            if j not in seen:
+                ve.wait_ge(sem["m%d" % j], 1)
+                seen.append(j)
+            if kind == "p":
+                fold(T.pacc[:, 0:ws], T["ps%d" % j][:, 0:ws], sem.vp, kp)
+                kp += 1
+            else:
+                fold(T.acc[:, 0:wr], T["ps%d" % j][:, ws:ws + wr], sem.vo, k)
+                k += 1
+        g.wait_ge(sem.vp, kp)
+        round2(T.pland[:, 0:ws], T.pacc[:, 0:ws], sem.pa)
+
+    g.sync.wait_ge(sem.vo, k)
+    g.sync.dma_start(T.y[:, 0:wr], T.acc[:, 0:wr]).then_inc(sem.st, 16)
+    g.sync.wait_ge(sem.st, 16)
+    g.wait_ge(sem.sent, sent[0])

@@ -4,16 +4,19 @@ from concourse.mybir import AluOpType
 N, M, TK = 6, 128, 256
 
 SCRATCH = {
-    "cat": ("sbuf", [128, M + M + TK], "bfloat16"),
+    "xb": ("sbuf", [128, M + TK], "bfloat16"),
     "wl": ("sbuf", [128, N * M], "bfloat16"),
     "pacc": ("sbuf", [128, M], "bfloat16"),
     "pland": ("sbuf", [128, M], "bfloat16"),
     "acc": ("sbuf", [128, TK], "bfloat16"),
+    "q0": ("psum", [128, 512], "float32"),
+    "q1": ("psum", [128, 512], "float32"),
 }
 for _j in range(N):
     SCRATCH["ps%d" % _j] = ("psum", [128, 512], "float32")
 
-SEMAPHORES = ["ldw", "ldx", "sent", "pa", "vp", "vo", "st"] + ["a%d" % j for j in range(N)] + ["m%d" % j for j in range(N)]
+SEMAPHORES = (["ldw", "ldx", "sent", "ax", "pa", "vp", "vo", "st", "n0", "n1"] + ["a%d" % j for j in range(N)]
+              + ["m%d" % j for j in range(N)])
 
 
 def _pop(mask):
@@ -69,17 +72,15 @@ def _plan(cores, wid, topo):
         plain = [b for b in wide if b != j and near[j][b] and not (j in narrow and partner[j] == b)]
         plain.sort(key=lambda d: links(j, d))
         tg = relay + plain
-        cj = []
-        if j in narrow:
-            cj.append([("cat", 0, M + wid[j], [partner[j]], topo.mask(cores[j], cores[partner[j]]))])
-            src = ("cat", 0, M)
-        else:
-            src = ("wl", j * M, (j + 1) * M)
         common = topo.mask(cores[j], cores[tg[0]])
         for d in tg:
             common &= topo.mask(cores[j], cores[d])
-        cj.append([(src[0], src[1], src[2], [d], mk) for d, mk in zip(tg, _split(common, len(tg)))])
-        calls[j] = cj
+        awaited = [("w", d, mk) for d, mk in zip(tg, _split(common, len(tg)))]
+        if j in narrow:
+            full = topo.mask(cores[j], cores[partner[j]])
+            calls[j] = [[("x", partner[j], _split(full, 2)[0])], awaited, [("w", partner[j], full)]]
+        else:
+            calls[j] = [awaited]
     return dict(near=near, links=links, narrow=narrow, wide=wide, far=far, partner=partner, calls=calls)
 
 
@@ -100,25 +101,20 @@ def rank_program(g, core, T, topo):
     def slot(j):
         return T.wl[:, j * M:(j + 1) * M]
 
-    def inc1(j):
-        return sum(_pop(t[4]) for c in calls[j] for t in c if r in t[3])
-
-    def dst_id(d):
-        rid, pid = topo.addr(cores[d], core)
-        return DstId(rid=rid, pnc=pid)
+    def inc1(j, what="w"):
+        return sum(_pop(t[2]) for c in calls[j] for t in c if t[1] == r and t[0] == what)
 
     sent = [0]
 
-    def round1():
-        for c in calls[r]:
-            trs = []
-            for buf, c0, c1, ds, mk in c:
-                whole = buf == "cat" and c1 > M
-                out = T.cat[:, c0:c1] if whole else slot(r)
-                trs.append(RemoteDMATransfer(dst_ids=[dst_id(d) for d in ds], dma_engine_mask=mk, remote_sem=arr(r),
-                                             srcs=[T[buf][:, c0:c1]], dsts=[out for d in ds], alu_op=0))
-                sent[0] += _pop(mk)
-            g.remote_dma_fused(trs, local_sem=sem.sent)
+    def issue(c):
+        trs = []
+        for what, d, mk in c:
+            rid, pid = topo.addr(cores[d], core)
+            ap = T.xb[:, 0:wr] if what == "x" else slot(r)
+            trs.append(RemoteDMATransfer(dst_ids=[DstId(rid=rid, pnc=pid)], dma_engine_mask=mk,
+                                         remote_sem=sem.ax if what == "x" else arr(r), srcs=[ap], dsts=[ap], alu_op=0))
+            sent[0] += _pop(mk)
+        g.remote_dma_fused(trs, local_sem=sem.sent)
 
     def round2(out_ap, in_ap, rsem):
         rid, pid = topo.addr(cores[p], core)
@@ -137,57 +133,82 @@ def rank_program(g, core, T, topo):
 
     if is_narrow:
         rel = P["far"][p]
-        g.sync.dma_start(T.cat[:, 0:M], T.w[:, :]).then_inc(sem.ldw, 16)
-        g.scalar.dma_start(T.cat[:, M:M + wr], T.x[:, 0:wr]).then_inc(sem.ldx, 16)
-        g.wait_ge(sem.ldw, 16)
+        g.scalar.dma_start(T.xb[:, 0:wr], T.x[:, 0:wr]).then_inc(sem.ldx, 16)
+        g.sync.dma_start(slot(r), T.w[:, :]).then_inc(sem.ldw, 16)
         g.wait_ge(sem.ldx, 16)
-        round1()
+        issue(calls[r][0])
+        g.wait_ge(sem.ldw, 16)
+        for c in calls[r][1:]:
+            issue(c)
         for f in rel:
             g.wait_ge(arr(f), inc1(f))
             round2(slot(f), slot(f), arr(f))
-        x = T.cat[:, M:M + wr]
+        x = T.xb[:, 0:wr]
         te.wait_ge(sem.ldw, 16)
         te.wait_ge(sem.ldx, 16)
-        te.matmul(T["ps%d" % r][:, 0:wr], T.cat[:, 0:M], x, start=True, stop=True).then_inc(sem["m%d" % r], 1)
+        te.matmul(T["ps%d" % r][:, 0:wr], slot(r), x, start=True, stop=True).then_inc(sem["m%d" % r], 1)
         for f in rel:
             te.wait_ge(arr(f), inc1(f))
             te.matmul(T["ps%d" % f][:, 0:wr], slot(f), x, start=True, stop=True).then_inc(sem["m%d" % f], 1)
+        mine = [r] + rel
         k = 0
-        for j in [r] + rel:
+        for j in mine:
             ve.wait_ge(sem["m%d" % j], 1)
-            fold(T.acc[:, 0:wr], T["ps%d" % j][:, 0:wr], sem.vo, k)
+            if k == 0:
+                ve.tensor_copy(T.acc[:, 0:wr], T["ps%d" % j][:, 0:wr]).then_inc(sem.vo, 1)
+            else:
+                ve.wait_ge(sem.vo, k)
+                out = T.q0[:, 0:wr] if j == mine[-1] else T.acc[:, 0:wr]
+                ve.tensor_tensor(out, T["ps%d" % j][:, 0:wr], T.acc[:, 0:wr], AluOpType.max).then_inc(sem.vo, 1)
             k += 1
         ve.wait_ge(sem.pa, inc2)
-        fold(T.acc[:, 0:wr], T.pland[:, 0:wr], sem.vo, k)
+        ve.wait_ge(sem.vo, k)
+        held = T.q0[:, 0:wr] if len(mine) > 1 else T.acc[:, 0:wr]
+        ve.tensor_tensor(T.acc[:, 0:wr], held, T.pland[:, 0:wr], AluOpType.max).then_inc(sem.vo, 1)
         k += 1
     else:
         ws = wid[p]
         far = P["far"][r]
         g.sync.dma_start(slot(r), T.w[:, :]).then_inc(sem.ldw, 16)
-        g.scalar.dma_start(T.cat[:, M + ws:M + ws + wr], T.x[:, 0:wr]).then_inc(sem.ldx, 16)
+        g.scalar.dma_start(T.xb[:, ws:ws + wr], T.x[:, 0:wr]).then_inc(sem.ldx, 16)
         g.wait_ge(sem.ldw, 16)
-        round1()
+        for c in calls[r]:
+            issue(c)
         oth = [j for j in range(len(cores)) if j not in (r, p) and j not in far]
         oth.sort(key=lambda j: (j in P["narrow"], P["links"](j, r)))
-        both = T.cat[:, M:M + ws + wr]
-        own = T.cat[:, M + ws:M + ws + wr]
+        last = oth[-2:]
+        both = T.xb[:, 0:ws + wr]
+        his = T.xb[:, 0:ws]
+        own = T.xb[:, ws:ws + wr]
         te.wait_ge(sem.ldw, 16)
         te.wait_ge(sem.ldx, 16)
-        te.wait_ge(arr(p), inc1(p))
+        te.wait_ge(sem.ax, inc1(p, "x"))
         te.matmul(T["ps%d" % r][:, 0:ws + wr], slot(r), both, start=True, stop=True).then_inc(sem["m%d" % r], 1)
-        te.matmul(T["ps%d" % p][:, ws:ws + wr], T.cat[:, 0:M], own, start=True, stop=True).then_inc(sem["m%d" % p], 1)
-        for j in oth:
+        for j in oth[:-2]:
             te.wait_ge(arr(j), inc1(j))
             te.matmul(T["ps%d" % j][:, 0:ws + wr], slot(j), both, start=True, stop=True).then_inc(sem["m%d" % j], 1)
+        for i, j in enumerate(last):
+            te.wait_ge(arr(j), inc1(j))
+            te.matmul(T["q%d" % i][:, 0:ws], slot(j), his, start=True, stop=True).then_inc(sem["n%d" % i], 1)
+        for j in last:
+            te.matmul(T["ps%d" % j][:, ws:ws + wr], slot(j), own, start=True, stop=True).then_inc(sem["m%d" % j], 1)
+        te.wait_ge(arr(p), inc1(p))
+        te.matmul(T["ps%d" % p][:, ws:ws + wr], slot(p), own, start=True, stop=True).then_inc(sem["m%d" % p], 1)
         for f in far:
             te.wait_ge(arr(f), inc2)
             te.matmul(T["ps%d" % f][:, ws:ws + wr], slot(f), own, start=True, stop=True).then_inc(sem["m%d" % f], 1)
-        seq = [("p", r), ("o", r), ("o", p)]
+        seq = [("p", r), ("o", r)]
         for j in oth[:-2]:
             seq += [("p", j), ("o", j)]
-        seq += [("p", j) for j in oth[-2:]] + [("o", j) for j in oth[-2:]] + [("o", f) for f in far]
+        seq += [("p", j) for j in last] + [("o", j) for j in last] + [("o", p)] + [("o", f) for f in far]
         kp, k, seen = 0, 0, []
         for kind, j in seq:
+            if kind == "p" and j in last:
+                i = last.index(j)
+                ve.wait_ge(sem["n%d" % i], 1)
+                fold(T.pacc[:, 0:ws], T["q%d" % i][:, 0:ws], sem.vp, kp)
+                kp += 1
+                continue
             if j not in seen:
                 ve.wait_ge(sem["m%d" % j], 1)
                 seen.append(j)

from concourse.bass import DstId, RemoteDMATransfer
from concourse.mybir import AluOpType

N, M, TK = 6, 128, 256

SCRATCH = {
    "xb": ("sbuf", [128, M + TK], "bfloat16"),
    "wl": ("sbuf", [128, N * M], "bfloat16"),
    "pacc": ("sbuf", [128, M], "bfloat16"),
    "pland": ("sbuf", [128, M], "bfloat16"),
    "acc": ("sbuf", [128, TK], "bfloat16"),
    "q0": ("psum", [128, 512], "float32"),
    "q1": ("psum", [128, 512], "float32"),
}
for _j in range(N):
    SCRATCH["ps%d" % _j] = ("psum", [128, 512], "float32")

SEMAPHORES = (["ldw", "ldx", "sent", "ax", "pa", "vp", "vo", "st", "n0", "n1"] + ["a%d" % j for j in range(N)]
              + ["m%d" % j for j in range(N)])


def _pop(mask):
    return bin(mask).count("1")


def _split(mask, k):
    es = [e for e in range(mask.bit_length()) if (mask >> e) & 1]
    per = 1
    while per * 2 * k <= len(es):
        per *= 2
    return [sum(1 << e for e in es[i * per:(i + 1) * per]) for i in range(k)]


def _plan(cores, wid, topo):
    n = len(cores)
    R = range(n)
    near = [[a != b and topo.may_write(cores[a], cores[b]) and topo.may_write(cores[b], cores[a]) for b in R] for a in R]

    def links(a, b):
        ca, cb = cores[a], cores[b]
        if topo.mates(ca, cb) or topo.same_plane(ca, cb):
            return 1
        if topo.rack(topo.host(ca)) != topo.rack(topo.host(cb)) and topo.chip(ca) == topo.chip(cb):
            return 1
        return 2

    narrow = [r for r in R if wid[r] <= M]
    wide = [r for r in R if wid[r] > M]
    far = dict((b, [j for j in R if j != b and not near[j][b]]) for b in wide)
    best = [None, None]

    def match(i, used, cost, pairs):
        if i == len(narrow):
            if best[0] is None or cost < best[0]:
                best[0], best[1] = cost, list(pairs)
            return
        s = narrow[i]
        for b in wide:
            if b in used or not near[b][s] or any(not near[f][s] for f in far[b]):
                continue
            match(i + 1, used + [b], cost + links(b, s), pairs + [(s, b)])

    match(0, [], 0, [])
    assert best[1] is not None and len(narrow) == len(wide)
    partner = {}
    for s, b in best[1]:
        partner[s], partner[b] = b, s

    calls = {}
    for j in R:
        relay = [s for s in narrow if s != j and j in far[partner[s]]]
        plain = [b for b in wide if b != j and near[j][b] and not (j in narrow and partner[j] == b)]
        plain.sort(key=lambda d: links(j, d))
        tg = relay + plain
        common = topo.mask(cores[j], cores[tg[0]])
        for d in tg:
            common &= topo.mask(cores[j], cores[d])
        awaited = [("w", d, mk) for d, mk in zip(tg, _split(common, len(tg)))]
        if j in narrow:
            full = topo.mask(cores[j], cores[partner[j]])
            calls[j] = [[("x", partner[j], _split(full, 2)[0])], awaited, [("w", partner[j], full)]]
        else:
            calls[j] = [awaited]
    return dict(near=near, links=links, narrow=narrow, wide=wide, far=far, partner=partner, calls=calls)


def rank_program(g, core, T, topo):
    r = T.rank_of(core)
    if r is None:
        return
    cores, wid = list(T.cores), list(T.tables["WID"])
    P = _plan(cores, wid, topo)
    sem, partner, calls = T.sem, P["partner"], P["calls"]
    wr, p = wid[r], partner[r]
    is_narrow = r in P["narrow"]
    te, ve = g.tensor, g.vector

    def arr(j):
        return sem["a%d" % j]

    def slot(j):
        return T.wl[:, j * M:(j + 1) * M]

    def inc1(j, what="w"):
        return sum(_pop(t[2]) for c in calls[j] for t in c if t[1] == r and t[0] == what)

    sent = [0]

    def issue(c):
        trs = []
        for what, d, mk in c:
            rid, pid = topo.addr(cores[d], core)
            ap = T.xb[:, 0:wr] if what == "x" else slot(r)
            trs.append(RemoteDMATransfer(dst_ids=[DstId(rid=rid, pnc=pid)], dma_engine_mask=mk,
                                         remote_sem=sem.ax if what == "x" else arr(r), srcs=[ap], dsts=[ap], alu_op=0))
            sent[0] += _pop(mk)
        g.remote_dma_fused(trs, local_sem=sem.sent)

    def round2(out_ap, in_ap, rsem):
        rid, pid = topo.addr(cores[p], core)
        mk = topo.mask(core, cores[p])
        g.remote_dma(out_ap, in_ap, rsem, sem.sent, pid, rid, mk)
        sent[0] += _pop(mk)

    inc2 = _pop(topo.mask(cores[p], core))

    def fold(out, ps_ap, chain, k):
        if k == 0:
            ve.tensor_copy(out, ps_ap).then_inc(chain, 1)
        else:
            ve.wait_ge(chain, k)
            ve.tensor_tensor(out, ps_ap, out, AluOpType.max).then_inc(chain, 1)

    if is_narrow:
        rel = P["far"][p]
        g.scalar.dma_start(T.xb[:, 0:wr], T.x[:, 0:wr]).then_inc(sem.ldx, 16)
        g.sync.dma_start(slot(r), T.w[:, :]).then_inc(sem.ldw, 16)
        g.wait_ge(sem.ldx, 16)
        issue(calls[r][0])
        g.wait_ge(sem.ldw, 16)
        for c in calls[r][1:]:
            issue(c)
        for f in rel:
            g.wait_ge(arr(f), inc1(f))
            round2(slot(f), slot(f), arr(f))
        x = T.xb[:, 0:wr]
        te.wait_ge(sem.ldw, 16)
        te.wait_ge(sem.ldx, 16)
        te.matmul(T["ps%d" % r][:, 0:wr], slot(r), x, start=True, stop=True).then_inc(sem["m%d" % r], 1)
        for f in rel:
            te.wait_ge(arr(f), inc1(f))
            te.matmul(T["ps%d" % f][:, 0:wr], slot(f), x, start=True, stop=True).then_inc(sem["m%d" % f], 1)
        mine = [r] + rel
        k = 0
        for j in mine:
            ve.wait_ge(sem["m%d" % j], 1)
            if k == 0:
                ve.tensor_copy(T.acc[:, 0:wr], T["ps%d" % j][:, 0:wr]).then_inc(sem.vo, 1)
            else:
                ve.wait_ge(sem.vo, k)
                out = T.q0[:, 0:wr] if j == mine[-1] else T.acc[:, 0:wr]
                ve.tensor_tensor(out, T["ps%d" % j][:, 0:wr], T.acc[:, 0:wr], AluOpType.max).then_inc(sem.vo, 1)
            k += 1
        ve.wait_ge(sem.pa, inc2)
        ve.wait_ge(sem.vo, k)
        held = T.q0[:, 0:wr] if len(mine) > 1 else T.acc[:, 0:wr]
        ve.tensor_tensor(T.acc[:, 0:wr], held, T.pland[:, 0:wr], AluOpType.max).then_inc(sem.vo, 1)
        k += 1
    else:
        ws = wid[p]
        far = P["far"][r]
        g.sync.dma_start(slot(r), T.w[:, :]).then_inc(sem.ldw, 16)
        g.scalar.dma_start(T.xb[:, ws:ws + wr], T.x[:, 0:wr]).then_inc(sem.ldx, 16)
        g.wait_ge(sem.ldw, 16)
        for c in calls[r]:
            issue(c)
        oth = [j for j in range(len(cores)) if j not in (r, p) and j not in far]
        oth.sort(key=lambda j: (j in P["narrow"], P["links"](j, r)))
        last = oth[-2:]
        both = T.xb[:, 0:ws + wr]
        his = T.xb[:, 0:ws]
        own = T.xb[:, ws:ws + wr]
        te.wait_ge(sem.ldw, 16)
        te.wait_ge(sem.ldx, 16)
        te.wait_ge(sem.ax, inc1(p, "x"))
        te.matmul(T["ps%d" % r][:, 0:ws + wr], slot(r), both, start=True, stop=True).then_inc(sem["m%d" % r], 1)
        for j in oth[:-2]:
            te.wait_ge(arr(j), inc1(j))
            te.matmul(T["ps%d" % j][:, 0:ws + wr], slot(j), both, start=True, stop=True).then_inc(sem["m%d" % j], 1)
        for i, j in enumerate(last):
            te.wait_ge(arr(j), inc1(j))
            te.matmul(T["q%d" % i][:, 0:ws], slot(j), his, start=True, stop=True).then_inc(sem["n%d" % i], 1)
        for j in last:
            te.matmul(T["ps%d" % j][:, ws:ws + wr], slot(j), own, start=True, stop=True).then_inc(sem["m%d" % j], 1)
        te.wait_ge(arr(p), inc1(p))
        te.matmul(T["ps%d" % p][:, ws:ws + wr], slot(p), own, start=True, stop=True).then_inc(sem["m%d" % p], 1)
        for f in far:
            te.wait_ge(arr(f), inc2)
            te.matmul(T["ps%d" % f][:, ws:ws + wr], slot(f), own, start=True, stop=True).then_inc(sem["m%d" % f], 1)
        seq = [("p", r), ("o", r)]
        for j in oth[:-2]:
            seq += [("p", j), ("o", j)]
        seq += [("p", j) for j in last] + [("o", j) for j in last] + [("o", p)] + [("o", f) for f in far]
        kp, k, seen = 0, 0, []
        for kind, j in seq:
            if kind == "p" and j in last:
                i = last.index(j)
                ve.wait_ge(sem["n%d" % i], 1)
                fold(T.pacc[:, 0:ws], T["q%d" % i][:, 0:ws], sem.vp, kp)
                kp += 1
                continue
            if j not in seen:
                ve.wait_ge(sem["m%d" % j], 1)
                seen.append(j)
            if kind == "p":
                fold(T.pacc[:, 0:ws], T["ps%d" % j][:, 0:ws], sem.vp, kp)
                kp += 1
            else:
                fold(T.acc[:, 0:wr], T["ps%d" % j][:, ws:ws + wr], sem.vo, k)
                k += 1
        g.wait_ge(sem.vp, kp)
        round2(T.pland[:, 0:ws], T.pacc[:, 0:ws], sem.pa)

    g.sync.wait_ge(sem.vo, k)
    g.sync.dma_start(T.y[:, 0:wr], T.acc[:, 0:wr]).then_inc(sem.st, 16)
    g.sync.wait_ge(sem.st, 16)
    g.wait_ge(sem.sent, sent[0])
